import numpy as np
import ml_dtypes


def mxq(x, axis, fmt="e4m3"):
    dtype, down = {"e4m3": (ml_dtypes.float8_e4m3fn, 7), "e5m2": (ml_dtypes.float8_e5m2, 14)}[fmt]
    v = np.moveaxis(np.asarray(x, np.float32).astype(ml_dtypes.bfloat16).astype(np.float64), axis, -1)
    blocks = v.reshape(v.shape[:-1] + (-1, 32))
    amax = np.abs(blocks).max(-1, keepdims=True)
    byte = np.maximum(np.where(amax > 0, np.frexp(amax)[1] - 1 + 127, 0) - down, 1)
    scale = np.exp2(byte - 127.0)
    codes = (blocks / scale).astype(np.float32).astype(dtype).astype(np.float64)
    return np.moveaxis((codes * scale).reshape(v.shape), -1, axis)


WIDE = False


def mx_kscale(k):
    if not WIDE:
        return np.ones(k)
    levels = np.array([10, -10, 5, -5, 0])
    if k % 512:
        return np.exp2(np.random.permutation(np.resize(levels, k // 32))).repeat(32)
    a = np.empty((k // 512, 16))
    for p in range(k // 512):
        a[p, :8] = np.random.permutation(np.resize(levels, 8))
        for g in range(8):
            far = levels[np.abs(levels - a[p, g]) >= 10]
            a[p, g + 8] = far[np.random.randint(len(far))]
    return np.exp2(a.ravel()).repeat(32)


def f64(x):
    return np.asarray(x).astype(np.float64)


def striped(idx):
    return np.tile(idx.reshape(-1, 16).T, (8, 1)).astype(np.uint16)


def unstriped(offs):
    return offs[:16].T.reshape(-1).astype(np.int64)


def gelu(v):
    return 0.5 * v * (1.0 + np.tanh(np.sqrt(2.0 / np.pi) * (v + 0.044715 * v**3)))


K, T, S, J, H, N = 1024, 2048, 512, 512, 512, 128


def setup_inputs():
    n = np.random.standard_normal
    s = mx_kscale(K)[:, None]
    u = mx_kscale(H)
    r = mx_kscale(J)[:, None]
    return {
        "xT": (n((K, T)) * s).astype(np.float32),
        "eT": (n((J, S)) * r).astype(np.float32),
        "w1": (n((K, H)) / np.sqrt(K) / s * u).astype(np.float32),
        "w3": (n((J, H)) / np.sqrt(J) / r).astype(np.float32),
        "w2": (n((H, N)) / np.sqrt(H) / u[:, None]).astype(np.float32),
        "offs": striped(np.random.permutation(T)[:S]),
    }


def reference(xT, eT, w1, w3, w2, offs):
    c = mxq(f64(w1), 0, "e4m3").T @ mxq(f64(xT)[:, unstriped(offs)], 0, "e4m3")
    z = c * gelu(mxq(f64(w3), 0, "e4m3").T @ mxq(f64(eT), 0, "e4m3"))
    return mxq(f64(w2), 0, "e4m3").T @ mxq(z, 0, "e4m3")

@@ -1,0 +1,198 @@
+from contextlib import ExitStack
+
+import concourse.mybir as mybir
+
+K, T, S, J, H, N = 1024, 2048, 512, 512, 512, 128
+FLOPS = 2 * (K * H * S + J * H * S + H * N * S)
+
+F32 = mybir.dt.float32
+BF16 = mybir.dt.bfloat16
+U32 = mybir.dt.uint32
+U16 = mybir.dt.uint16
+U8 = mybir.dt.uint8
+FP8X4 = mybir.dt.float8_e4m3fn_x4
+GELU = mybir.ActivationFunctionType.Gelu_apprx_tanh
+MULT = mybir.AluOpType.mult
+
+P = 128
+PACK = 4
+PASSES = K // (P * PACK)
+HALF = S // 2
+CHUNK = 128
+CHUNKS = S // CHUNK
+PIECES = [(0, 128), (128, 256), (256, 384), (384, 448), (448, 512)]
+
+
+def tile_picked_schnet_gelu_e_kernel(tc, xT, eT, w1, w3, w2, offs, out):
+    nc = tc.nc
+    with ExitStack() as ctx:
+        keep = ctx.enter_context(tc.tile_pool(name="keep", bufs=1))
+        psum = ctx.enter_context(tc.psum_pool(name="psum", bufs=1))
+
+        def sbuf(shape, dtype, name):
+            return keep.tile(shape, dtype, name=name, align_bytes=64)
+
+        lists = keep.tile([P, S // 16], U16, name="lists")
+
+        warm = sbuf([P, 2], F32, "warm")
+        nc.vector.memset(warm[:], 0.0)
+        warm_out = sbuf([P, 2], F32, "warm_out")
+        nc.scalar.activation(warm_out[:], warm[:], GELU)
+
+        def rows(ap, s):
+            return ap[s * P * PACK : (s + 1) * P * PACK, :].rearrange("(p j) c -> p j c", j=PACK)
+
+        w1_raw = [sbuf([P, PACK, H], F32, f"w1_raw{s}") for s in range(PASSES)]
+        w3_raw = [sbuf([P, PACK, H // 2], F32, f"w3_raw{h}") for h in range(2)]
+        w2_raw = sbuf([P, PACK, N], F32, "w2_raw")
+        x_raw = [[sbuf([P, T], F32, f"x_raw{s}_{j}") for j in range(PACK)] for s in range(PASSES)]
+        e_cols = [(0, 256), (256, 384), (384, 512)]
+        e_raw = [sbuf([P, PACK, b - a], F32, f"e_raw{a}") for a, b in e_cols]
+
+        nc.sync.dma_start(out=w1_raw[0][:], in_=rows(w1, 0))
+        nc.sync.dma_start(lists[:], offs)
+        nc.sync.dma_start(out=w1_raw[1][:], in_=rows(w1, 1))
+        for s in range(PASSES):
+            for j in range(PACK):
+                nc.sync.dma_start(out=x_raw[s][j][:], in_=rows(xT, s)[:, j, :])
+        for h in range(2):
+            nc.sync.dma_start(out=w3_raw[h][:], in_=rows(w3, 0)[:, :, h * H // 2 : (h + 1) * H // 2])
+        for i, (a, b) in enumerate(e_cols):
+            nc.sync.dma_start(out=e_raw[i][:], in_=rows(eT, 0)[:, :, a:b])
+        nc.sync.dma_start(out=w2_raw[:], in_=rows(w2, 0))
+
+        def quantize(codes, scales, grouped):
+            nc.vector.quantize_mx(out=codes.bitcast(FP8X4), scales=scales, in_=grouped.rearrange("p c j -> p (c j)"))
+
+        def mx(acc, lhs, rhs, start, stop):
+            nc.tensor.matmul_mx(
+                out=acc, lhsT=lhs[0].bitcast(FP8X4), lhsT_scale=lhs[1],
+                rhs=rhs[0].bitcast(FP8X4), rhs_scale=rhs[1], start=start, stop=stop,
+            )
+
+        def permuted(grouped, m0, m1):
+            return grouped.rearrange("p (t m) j -> p m t j", t=PACK)[:, m0:m1, :, :]
+
+        def gather(s, j, a, b):
+            nc.vector.tensor_copy(x_g[s][:, a:b, j], x_raw[s][j][:].indirect(lists[:, a // 16 : b // 16]))
+
+        w1_q = [sbuf([P, H], U32, f"w1_q{s}") for s in range(PASSES)]
+        w1_s = [sbuf([P, H], U8, f"w1_s{s}") for s in range(PASSES)]
+        w1_g = [sbuf([P, H, PACK], BF16, f"w1_g{s}") for s in range(PASSES)]
+        for s in range(PASSES):
+            nc.scalar.copy(permuted(w1_g[s][:], 0, 128), w1_raw[s][:].rearrange("p j (m t) -> p m t j", t=PACK))
+
+        x_g = [sbuf([P, S, PACK], BF16, f"x_g{s}") for s in range(PASSES)]
+        x_q = [[sbuf([P, HALF], U32, f"x_q{s}_{h}") for h in range(2)] for s in range(PASSES)]
+        x_s = [[sbuf([P, HALF], U8, f"x_s{s}_{h}") for h in range(2)] for s in range(PASSES)]
+        w3_g = sbuf([P, H, PACK], BF16, "w3_g")
+        w3_q = sbuf([P, H], U32, "w3_q")
+        w3_s = sbuf([P, H], U8, "w3_s")
+
+        def quantize_x(s, h):
+            quantize(x_q[s][h][:], x_s[s][h][:], x_g[s][:, h * HALF : (h + 1) * HALF, :])
+
+        gather(0, 0, 0, S)
+        quantize(w1_q[0][:], w1_s[0][:], w1_g[0][:])
+        gather(0, 1, 0, S)
+        quantize(w1_q[1][:], w1_s[1][:], w1_g[1][:])
+        gather(0, 2, 0, S)
+        gather(0, 3, 0, S)
+        gather(1, 0, 0, S)
+        quantize_x(0, 0)
+        quantize_x(0, 1)
+        gather(1, 1, 0, S)
+        gather(1, 2, 0, S)
+        gather(1, 3, 0, HALF)
+        gather(1, 3, HALF, S)
+        quantize_x(1, 0)
+        quantize_x(1, 1)
+
+        def w3_copy(copy, h):
+            copy(permuted(w3_g[:], h * 64, (h + 1) * 64), w3_raw[h][:].rearrange("p j (m t) -> p m t j", t=PACK))
+
+        w3_copy(nc.scalar.copy, 0)
+        w3_copy(nc.vector.tensor_copy, 1)
+        quantize(w3_q[:], w3_s[:], w3_g[:])
+
+        c_ps = [psum.tile([P, PACK, CHUNK], F32, name=f"c_ps{n}", tag=f"bank{n}") for n in range(CHUNKS)]
+        for n in range(CHUNKS):
+            h, col = n // 2, slice((n % 2) * CHUNK, (n % 2 + 1) * CHUNK)
+            for t in range(PACK):
+                m = slice(t * P, (t + 1) * P)
+                for s in range(PASSES):
+                    mx(c_ps[n][:, t, :], (w1_q[s][:, m], w1_s[s][:, m]), (x_q[s][h][:, col], x_s[s][h][:, col]),
+                       s == 0, s == PASSES - 1)
+
+        e_g = [sbuf([P, b - a, PACK], BF16, f"e_g{a}") for a, b in e_cols]
+        e_q = [sbuf([P, b - a], U32, f"e_q{a}") for a, b in e_cols]
+        e_s = [sbuf([P, b - a], U8, f"e_s{a}") for a, b in e_cols]
+        w2_g = sbuf([P, N, PACK], BF16, "w2_g")
+        w2_q = sbuf([P, N], U32, "w2_q")
+        w2_s = sbuf([P, N], U8, "w2_s")
+        width = [b - a for a, b in PIECES]
+        g_sb = [sbuf([P, w, PACK], F32, f"g_sb{n}") for n, w in enumerate(width)]
+        z_g = [sbuf([P, w, PACK], BF16, f"z_g{n}") for n, w in enumerate(width)]
+        z_q = [sbuf([P, w], U32, f"z_q{n}") for n, w in enumerate(width)]
+        z_s = [sbuf([P, w], U8, f"z_s{n}") for n, w in enumerate(width)]
+        o_sb = sbuf([P, S], F32, "o_sb")
+
+        e_of = [0, 0, 1, 2, 2]
+        f_bank = [4, 5, 6, 7, 4]
+        o_bank = [0, 1, 2, 5, 3]
+
+        def e_copy(copy, i, a, b):
+            copy(e_g[i][:, a:b, :], e_raw[i][:, :, a:b].rearrange("p j c -> p c j"))
+
+        def e_quantize(i, a, b):
+            quantize(e_q[i][:, a:b], e_s[i][:, a:b], e_g[i][:, a:b, :])
+
+        def gelu(n):
+            i = e_of[n]
+            col = slice(PIECES[n][0] - e_cols[i][0], PIECES[n][1] - e_cols[i][0])
+            f_ps = psum.tile([P, PACK, width[n]], F32, name=f"f_ps{n}", tag=f"bank{f_bank[n]}")
+            for t in range(PACK):
+                m = slice(t * P, (t + 1) * P)
+                mx(f_ps[:, t, :], (w3_q[:, m], w3_s[:, m]), (e_q[i][:, col], e_s[i][:, col]), True, True)
+            nc.scalar.activation(g_sb[n][:], f_ps[:].rearrange("p t n -> p n t"), GELU)
+
+        def z(n):
+            c = c_ps[PIECES[n][0] // CHUNK]
+            a = PIECES[n][0] % CHUNK
+            nc.vector.tensor_tensor(z_g[n][:], c[:, :, a : a + width[n]].rearrange("p t n -> p n t"), g_sb[n][:], MULT)
+
+        def finish(n):
+            quantize(z_q[n][:], z_s[n][:], z_g[n][:])
+            cols = slice(*PIECES[n])
+            o_ps = psum.tile([P, width[n]], F32, name=f"o_ps{n}", tag=f"bank{o_bank[n]}")
+            mx(o_ps[:], (w2_q[:], w2_s[:]), (z_q[n][:], z_s[n][:]), True, True)
+            nc.scalar.copy(o_sb[:, cols], o_ps[:])
+            if n != 3:
+                cols = slice(384 if n == 4 else cols.start, cols.stop)
+                nc.sync.dma_start(out=out[:, cols], in_=o_sb[:, cols])
+
+        e_copy(nc.scalar.copy, 0, 0, 256)
+        e_quantize(0, 0, 256)
+        e_copy(nc.scalar.copy, 1, 0, 128)
+        gelu(0)
+        z(0)
+        e_quantize(1, 0, 128)
+        gelu(1)
+        z(1)
+        e_copy(nc.vector.tensor_copy, 2, 0, 64)
+        gelu(2)
+        e_copy(nc.vector.tensor_copy, 2, 64, 128)
+        e_quantize(2, 0, 64)
+        e_quantize(2, 64, 128)
+        gelu(3)
+        gelu(4)
+        nc.scalar.copy(w2_g[:], w2_raw[:].rearrange("p j c -> p c j"))
+        z(2)
+        quantize(w2_q[:], w2_s[:], w2_g[:])
+        finish(0)
+        finish(1)
+        z(3)
+        finish(2)
+        z(4)
+        finish(3)
+        finish(4)

@@ -20,7 +20,7 @@ PASSES = K // (P * PACK)
 HALF = S // 2
 CHUNK = 128
 CHUNKS = S // CHUNK
-PIECES = [(0, 128), (128, 256), (256, 384), (384, 448), (448, 512)]
+E_LOAD = 256
 
 
 def tile_picked_schnet_gelu_e_kernel(tc, xT, eT, w1, w3, w2, offs, out):
@@ -42,23 +42,21 @@ def tile_picked_schnet_gelu_e_kernel(tc, xT, eT, w1, w3, w2, offs, out):
         def rows(ap, s):
             return ap[s * P * PACK : (s + 1) * P * PACK, :].rearrange("(p j) c -> p j c", j=PACK)
 
-        w1_raw = [sbuf([P, PACK, H], F32, f"w1_raw{s}") for s in range(PASSES)]
-        w3_raw = [sbuf([P, PACK, H // 2], F32, f"w3_raw{h}") for h in range(2)]
-        w2_raw = sbuf([P, PACK, N], F32, "w2_raw")
-        x_raw = [[sbuf([P, T], F32, f"x_raw{s}_{j}") for j in range(PACK)] for s in range(PASSES)]
-        e_cols = [(0, 256), (256, 384), (384, 512)]
-        e_raw = [sbuf([P, PACK, b - a], F32, f"e_raw{a}") for a, b in e_cols]
-
-        nc.sync.dma_start(out=w1_raw[0][:], in_=rows(w1, 0))
+        w1_raw = sbuf([P, PASSES, PACK, H], F32, "w1_raw")
+        nc.sync.dma_start(out=w1_raw[:], in_=w1.rearrange("(s p j) c -> p s j c", p=P, j=PACK))
         nc.sync.dma_start(lists[:], offs)
-        nc.sync.dma_start(out=w1_raw[1][:], in_=rows(w1, 1))
-        for s in range(PASSES):
-            for j in range(PACK):
-                nc.sync.dma_start(out=x_raw[s][j][:], in_=rows(xT, s)[:, j, :])
-        for h in range(2):
-            nc.sync.dma_start(out=w3_raw[h][:], in_=rows(w3, 0)[:, :, h * H // 2 : (h + 1) * H // 2])
-        for i, (a, b) in enumerate(e_cols):
-            nc.sync.dma_start(out=e_raw[i][:], in_=rows(eT, 0)[:, :, a:b])
+        planes = {}
+        for s, j0, j1 in ((0, 0, 2), (0, 2, 4), (1, 0, 2), (1, 2, 3), (1, 3, 4)):
+            x_raw = sbuf([P, j1 - j0, T], F32, f"x_raw{s}{j0}")
+            nc.sync.dma_start(out=x_raw[:], in_=rows(xT, s)[:, j0:j1, :])
+            for j in range(j0, j1):
+                planes[s, j] = x_raw[:, j - j0, :]
+        w3_raw = sbuf([P, PACK, H], F32, "w3_raw")
+        nc.sync.dma_start(out=w3_raw[:], in_=rows(w3, 0))
+        e_raw = [sbuf([P, PACK, E_LOAD], F32, f"e_raw{i}") for i in range(S // E_LOAD)]
+        for i in range(S // E_LOAD):
+            nc.sync.dma_start(out=e_raw[i][:], in_=rows(eT, 0)[:, :, i * E_LOAD : (i + 1) * E_LOAD])
+        w2_raw = sbuf([P, PACK, N], F32, "w2_raw")
         nc.sync.dma_start(out=w2_raw[:], in_=rows(w2, 0))
 
         def quantize(codes, scales, grouped):
@@ -74,13 +72,13 @@ def tile_picked_schnet_gelu_e_kernel(tc, xT, eT, w1, w3, w2, offs, out):
             return grouped.rearrange("p (t m) j -> p m t j", t=PACK)[:, m0:m1, :, :]
 
         def gather(s, j, a, b):
-            nc.vector.tensor_copy(x_g[s][:, a:b, j], x_raw[s][j][:].indirect(lists[:, a // 16 : b // 16]))
+            nc.vector.tensor_copy(x_g[s][:, a:b, j], planes[s, j].indirect(lists[:, a // 16 : b // 16]))
 
         w1_q = [sbuf([P, H], U32, f"w1_q{s}") for s in range(PASSES)]
         w1_s = [sbuf([P, H], U8, f"w1_s{s}") for s in range(PASSES)]
         w1_g = [sbuf([P, H, PACK], BF16, f"w1_g{s}") for s in range(PASSES)]
         for s in range(PASSES):
-            nc.scalar.copy(permuted(w1_g[s][:], 0, 128), w1_raw[s][:].rearrange("p j (m t) -> p m t j", t=PACK))
+            nc.scalar.copy(permuted(w1_g[s][:], 0, 128), w1_raw[:, s, :, :].rearrange("p j (m t) -> p m t j", t=PACK))
 
         x_g = [sbuf([P, S, PACK], BF16, f"x_g{s}") for s in range(PASSES)]
         x_q = [[sbuf([P, HALF], U32, f"x_q{s}_{h}") for h in range(2)] for s in range(PASSES)]
@@ -108,15 +106,16 @@ def tile_picked_schnet_gelu_e_kernel(tc, xT, eT, w1, w3, w2, offs, out):
         quantize_x(1, 0)
         quantize_x(1, 1)
 
-        def w3_copy(copy, h):
-            copy(permuted(w3_g[:], h * 64, (h + 1) * 64), w3_raw[h][:].rearrange("p j (m t) -> p m t j", t=PACK))
+        def w3_copy(copy, m0, m1):
+            copy(permuted(w3_g[:], m0, m1), w3_raw[:, :, PACK * m0 : PACK * m1].rearrange("p j (m t) -> p m t j", t=PACK))
 
-        w3_copy(nc.scalar.copy, 0)
-        w3_copy(nc.vector.tensor_copy, 1)
+        w3_copy(nc.scalar.copy, 0, 44)
+        w3_copy(nc.vector.tensor_copy, 44, 128)
         quantize(w3_q[:], w3_s[:], w3_g[:])
 
         c_ps = [psum.tile([P, PACK, CHUNK], F32, name=f"c_ps{n}", tag=f"bank{n}") for n in range(CHUNKS)]
-        for n in range(CHUNKS):
+
+        def c(n):
             h, col = n // 2, slice((n % 2) * CHUNK, (n % 2 + 1) * CHUNK)
             for t in range(PACK):
                 m = slice(t * P, (t + 1) * P)
@@ -124,75 +123,76 @@ def tile_picked_schnet_gelu_e_kernel(tc, xT, eT, w1, w3, w2, offs, out):
                     mx(c_ps[n][:, t, :], (w1_q[s][:, m], w1_s[s][:, m]), (x_q[s][h][:, col], x_s[s][h][:, col]),
                        s == 0, s == PASSES - 1)
 
-        e_g = [sbuf([P, b - a, PACK], BF16, f"e_g{a}") for a, b in e_cols]
-        e_q = [sbuf([P, b - a], U32, f"e_q{a}") for a, b in e_cols]
-        e_s = [sbuf([P, b - a], U8, f"e_s{a}") for a, b in e_cols]
+        def per_chunk(shape, dtype, name):
+            return [sbuf(shape, dtype, f"{name}{n}") for n in range(CHUNKS)]
+
+        e_g = per_chunk([P, CHUNK, PACK], BF16, "e_g")
+        e_q = per_chunk([P, CHUNK], U32, "e_q")
+        e_s = per_chunk([P, CHUNK], U8, "e_s")
+        g_sb = per_chunk([P, CHUNK, PACK], F32, "g_sb")
+        z_g = per_chunk([P, CHUNK, PACK], BF16, "z_g")
+        z_q = per_chunk([P, CHUNK], U32, "z_q")
+        z_s = per_chunk([P, CHUNK], U8, "z_s")
+        o_sb = per_chunk([P, CHUNK], F32, "o_sb")
         w2_g = sbuf([P, N, PACK], BF16, "w2_g")
         w2_q = sbuf([P, N], U32, "w2_q")
         w2_s = sbuf([P, N], U8, "w2_s")
-        width = [b - a for a, b in PIECES]
-        g_sb = [sbuf([P, w, PACK], F32, f"g_sb{n}") for n, w in enumerate(width)]
-        z_g = [sbuf([P, w, PACK], BF16, f"z_g{n}") for n, w in enumerate(width)]
-        z_q = [sbuf([P, w], U32, f"z_q{n}") for n, w in enumerate(width)]
-        z_s = [sbuf([P, w], U8, f"z_s{n}") for n, w in enumerate(width)]
-        o_sb = sbuf([P, S], F32, "o_sb")
+        f_ps = [psum.tile([P, PACK, CHUNK], F32, name=f"f_ps{n}", tag=f"bank{4 + n}") for n in range(CHUNKS)]
 
-        e_of = [0, 0, 1, 2, 2]
-        f_bank = [4, 5, 6, 7, 4]
-        o_bank = [0, 1, 2, 5, 3]
+        def e_copy(copy, n):
+            per = E_LOAD // CHUNK
+            a = (n % per) * CHUNK
+            copy(e_g[n][:], e_raw[n // per][:, :, a : a + CHUNK].rearrange("p j c -> p c j"))
 
-        def e_copy(copy, i, a, b):
-            copy(e_g[i][:, a:b, :], e_raw[i][:, :, a:b].rearrange("p j c -> p c j"))
+        def e_quantize(n):
+            quantize(e_q[n][:], e_s[n][:], e_g[n][:])
 
-        def e_quantize(i, a, b):
-            quantize(e_q[i][:, a:b], e_s[i][:, a:b], e_g[i][:, a:b, :])
-
-        def gelu(n):
-            i = e_of[n]
-            col = slice(PIECES[n][0] - e_cols[i][0], PIECES[n][1] - e_cols[i][0])
-            f_ps = psum.tile([P, PACK, width[n]], F32, name=f"f_ps{n}", tag=f"bank{f_bank[n]}")
+        def f(n):
             for t in range(PACK):
                 m = slice(t * P, (t + 1) * P)
-                mx(f_ps[:, t, :], (w3_q[:, m], w3_s[:, m]), (e_q[i][:, col], e_s[i][:, col]), True, True)
-            nc.scalar.activation(g_sb[n][:], f_ps[:].rearrange("p t n -> p n t"), GELU)
+                mx(f_ps[n][:, t, :], (w3_q[:, m], w3_s[:, m]), (e_q[n][:], e_s[n][:]), True, True)
+
+        def gelu(n):
+            nc.scalar.activation(g_sb[n][:], f_ps[n][:].rearrange("p t n -> p n t"), GELU)
 
         def z(n):
-            c = c_ps[PIECES[n][0] // CHUNK]
-            a = PIECES[n][0] % CHUNK
-            nc.vector.tensor_tensor(z_g[n][:], c[:, :, a : a + width[n]].rearrange("p t n -> p n t"), g_sb[n][:], MULT)
+            nc.vector.tensor_tensor(z_g[n][:], c_ps[n][:].rearrange("p t n -> p n t"), g_sb[n][:], MULT)
 
-        def finish(n):
+        def project(copy, n):
             quantize(z_q[n][:], z_s[n][:], z_g[n][:])
-            cols = slice(*PIECES[n])
-            o_ps = psum.tile([P, width[n]], F32, name=f"o_ps{n}", tag=f"bank{o_bank[n]}")
+            o_ps = psum.tile([P, CHUNK], F32, name=f"o_ps{n}", tag=f"bank{n}")
             mx(o_ps[:], (w2_q[:], w2_s[:]), (z_q[n][:], z_s[n][:]), True, True)
-            nc.scalar.copy(o_sb[:, cols], o_ps[:])
-            if n != 3:
-                cols = slice(384 if n == 4 else cols.start, cols.stop)
-                nc.sync.dma_start(out=out[:, cols], in_=o_sb[:, cols])
+            copy(o_sb[n][:], o_ps[:])
+            nc.sync.dma_start(out=out[:, n * CHUNK : (n + 1) * CHUNK], in_=o_sb[n][:])
 
-        e_copy(nc.scalar.copy, 0, 0, 256)
-        e_quantize(0, 0, 256)
-        e_copy(nc.scalar.copy, 1, 0, 128)
+        scalar, vector = nc.scalar.copy, nc.vector.tensor_copy
+        e_copy(scalar, 0)
+        e_copy(vector, 1)
+        e_quantize(0)
+        e_quantize(1)
+        c(0)
+        f(0)
+        f(1)
+        c(1)
         gelu(0)
-        z(0)
-        e_quantize(1, 0, 128)
+        e_copy(scalar, 2)
+        e_copy(vector, 3)
+        e_quantize(3)
         gelu(1)
-        z(1)
-        e_copy(nc.vector.tensor_copy, 2, 0, 64)
+        e_quantize(2)
+        f(2)
+        c(2)
+        f(3)
+        c(3)
+        z(0)
         gelu(2)
-        e_copy(nc.vector.tensor_copy, 2, 64, 128)
-        e_quantize(2, 0, 64)
-        e_quantize(2, 64, 128)
+        z(1)
         gelu(3)
-        gelu(4)
-        nc.scalar.copy(w2_g[:], w2_raw[:].rearrange("p j c -> p c j"))
-        z(2)
+        vector(w2_g[:], w2_raw[:].rearrange("p j c -> p c j"))
         quantize(w2_q[:], w2_s[:], w2_g[:])
-        finish(0)
-        finish(1)
+        z(2)
+        project(scalar, 0)
+        project(scalar, 1)
         z(3)
-        finish(2)
-        z(4)
-        finish(3)
-        finish(4)
+        project(scalar, 2)
+        project(vector, 3)

@@ -42,15 +42,20 @@ def tile_picked_schnet_gelu_e_kernel(tc, xT, eT, w1, w3, w2, offs, out):
         def rows(ap, s):
             return ap[s * P * PACK : (s + 1) * P * PACK, :].rearrange("(p j) c -> p j c", j=PACK)
 
-        w1_raw = sbuf([P, PASSES, PACK, H], F32, "w1_raw")
-        nc.sync.dma_start(out=w1_raw[:], in_=w1.rearrange("(s p j) c -> p s j c", p=P, j=PACK))
-        nc.sync.dma_start(lists[:], offs)
+        w1_raw = [sbuf([P, PACK, H], F32, f"w1_raw{s}") for s in range(PASSES)]
         planes = {}
-        for s, j0, j1 in ((0, 0, 2), (0, 2, 4), (1, 0, 2), (1, 2, 3), (1, 3, 4)):
-            x_raw = sbuf([P, j1 - j0, T], F32, f"x_raw{s}{j0}")
-            nc.sync.dma_start(out=x_raw[:], in_=rows(xT, s)[:, j0:j1, :])
-            for j in range(j0, j1):
-                planes[s, j] = x_raw[:, j - j0, :]
+
+        def load_plane(s, j):
+            planes[s, j] = sbuf([P, T], F32, f"x_raw{s}{j}")
+            nc.sync.dma_start(out=planes[s, j][:], in_=rows(xT, s)[:, j, :])
+
+        nc.sync.dma_start(lists[:], offs)
+        for s in range(PASSES):
+            load_plane(s, 0)
+            load_plane(s, 1)
+            nc.sync.dma_start(out=w1_raw[s][:], in_=rows(w1, s))
+            load_plane(s, 2)
+            load_plane(s, 3)
         w3_raw = sbuf([P, PACK, H], F32, "w3_raw")
         nc.sync.dma_start(out=w3_raw[:], in_=rows(w3, 0))
         e_raw = [sbuf([P, PACK, E_LOAD], F32, f"e_raw{i}") for i in range(S // E_LOAD)]
@@ -72,14 +77,16 @@ def tile_picked_schnet_gelu_e_kernel(tc, xT, eT, w1, w3, w2, offs, out):
             return grouped.rearrange("p (t m) j -> p m t j", t=PACK)[:, m0:m1, :, :]
 
         def gather(s, j, a, b):
-            nc.vector.tensor_copy(x_g[s][:, a:b, j], planes[s, j].indirect(lists[:, a // 16 : b // 16]))
+            nc.vector.tensor_copy(picked[s][:, j, a:b], planes[s, j][:].indirect(lists[:, a // 16 : b // 16]))
 
         w1_q = [sbuf([P, H], U32, f"w1_q{s}") for s in range(PASSES)]
         w1_s = [sbuf([P, H], U8, f"w1_s{s}") for s in range(PASSES)]
         w1_g = [sbuf([P, H, PACK], BF16, f"w1_g{s}") for s in range(PASSES)]
-        for s in range(PASSES):
-            nc.scalar.copy(permuted(w1_g[s][:], 0, 128), w1_raw[:, s, :, :].rearrange("p j (m t) -> p m t j", t=PACK))
 
+        def w1_copy(s):
+            nc.scalar.copy(permuted(w1_g[s][:], 0, 128), w1_raw[s][:].rearrange("p j (m t) -> p m t j", t=PACK))
+
+        picked = [sbuf([P, PACK, S], F32, f"picked{s}") for s in range(PASSES)]
         x_g = [sbuf([P, S, PACK], BF16, f"x_g{s}") for s in range(PASSES)]
         x_q = [[sbuf([P, HALF], U32, f"x_q{s}_{h}") for h in range(2)] for s in range(PASSES)]
         x_s = [[sbuf([P, HALF], U8, f"x_s{s}_{h}") for h in range(2)] for s in range(PASSES)]
@@ -90,19 +97,29 @@ def tile_picked_schnet_gelu_e_kernel(tc, xT, eT, w1, w3, w2, offs, out):
         def quantize_x(s, h):
             quantize(x_q[s][h][:], x_s[s][h][:], x_g[s][:, h * HALF : (h + 1) * HALF, :])
 
+        def interleave(copy, s, j0, j1, a, b):
+            copy(x_g[s][:, a:b, j0:j1], picked[s][:, j0:j1, a:b].rearrange("p j n -> p n j"))
+
+        scalar, vector = nc.scalar.copy, nc.vector.tensor_copy
         gather(0, 0, 0, S)
-        quantize(w1_q[0][:], w1_s[0][:], w1_g[0][:])
         gather(0, 1, 0, S)
-        quantize(w1_q[1][:], w1_s[1][:], w1_g[1][:])
+        w1_copy(0)
         gather(0, 2, 0, S)
+        quantize(w1_q[0][:], w1_s[0][:], w1_g[0][:])
         gather(0, 3, 0, S)
+        interleave(scalar, 0, 0, 4, 0, S)
         gather(1, 0, 0, S)
+        gather(1, 1, 0, S)
         quantize_x(0, 0)
         quantize_x(0, 1)
-        gather(1, 1, 0, S)
+        w1_copy(1)
         gather(1, 2, 0, S)
+        interleave(scalar, 1, 0, 2, 0, S)
+        quantize(w1_q[1][:], w1_s[1][:], w1_g[1][:])
         gather(1, 3, 0, HALF)
+        interleave(scalar, 1, 2, 4, 0, HALF)
         gather(1, 3, HALF, S)
+        interleave(vector, 1, 2, 4, HALF, S)
         quantize_x(1, 0)
         quantize_x(1, 1)
 
@@ -165,7 +182,6 @@ def tile_picked_schnet_gelu_e_kernel(tc, xT, eT, w1, w3, w2, offs, out):
             copy(o_sb[n][:], o_ps[:])
             nc.sync.dma_start(out=out[:, n * CHUNK : (n + 1) * CHUNK], in_=o_sb[n][:])
 
-        scalar, vector = nc.scalar.copy, nc.vector.tensor_copy
         e_copy(scalar, 0)
         e_copy(vector, 1)
         e_quantize(0)

@@ -20,7 +20,8 @@ PASSES = K // (P * PACK)
 HALF = S // 2
 CHUNK = 128
 CHUNKS = S // CHUNK
-E_LOAD = 256
+E_LOAD = 128
+PIECES = [(0, 64), (64, 128), (128, 256), (256, 384), (384, 512)]
 
 
 def tile_picked_schnet_gelu_e_kernel(tc, xT, eT, w1, w3, w2, offs, out):
@@ -49,13 +50,12 @@ def tile_picked_schnet_gelu_e_kernel(tc, xT, eT, w1, w3, w2, offs, out):
             planes[s, j] = sbuf([P, T], F32, f"x_raw{s}{j}")
             nc.sync.dma_start(out=planes[s, j][:], in_=rows(xT, s)[:, j, :])
 
+        nc.sync.dma_start(out=w1_raw[0][:], in_=rows(w1, 0))
         nc.sync.dma_start(lists[:], offs)
+        nc.sync.dma_start(out=w1_raw[1][:], in_=rows(w1, 1))
         for s in range(PASSES):
-            load_plane(s, 0)
-            load_plane(s, 1)
-            nc.sync.dma_start(out=w1_raw[s][:], in_=rows(w1, s))
-            load_plane(s, 2)
-            load_plane(s, 3)
+            for j in range(PACK):
+                load_plane(s, j)
         w3_raw = sbuf([P, PACK, H], F32, "w3_raw")
         nc.sync.dma_start(out=w3_raw[:], in_=rows(w3, 0))
         e_raw = [sbuf([P, PACK, E_LOAD], F32, f"e_raw{i}") for i in range(S // E_LOAD)]
@@ -77,7 +77,8 @@ def tile_picked_schnet_gelu_e_kernel(tc, xT, eT, w1, w3, w2, offs, out):
             return grouped.rearrange("p (t m) j -> p m t j", t=PACK)[:, m0:m1, :, :]
 
         def gather(s, j, a, b):
-            nc.vector.tensor_copy(picked[s][:, j, a:b], planes[s, j][:].indirect(lists[:, a // 16 : b // 16]))
+            dst = picked[:, j, a:b] if s == 0 else x_g[s][:, a:b, j]
+            nc.vector.tensor_copy(dst, planes[s, j][:].indirect(lists[:, a // 16 : b // 16]))
 
         w1_q = [sbuf([P, H], U32, f"w1_q{s}") for s in range(PASSES)]
         w1_s = [sbuf([P, H], U8, f"w1_s{s}") for s in range(PASSES)]
@@ -86,7 +87,7 @@ def tile_picked_schnet_gelu_e_kernel(tc, xT, eT, w1, w3, w2, offs, out):
         def w1_copy(s):
             nc.scalar.copy(permuted(w1_g[s][:], 0, 128), w1_raw[s][:].rearrange("p j (m t) -> p m t j", t=PACK))
 
-        picked = [sbuf([P, PACK, S], F32, f"picked{s}") for s in range(PASSES)]
+        picked = sbuf([P, PACK, S], F32, "picked")
         x_g = [sbuf([P, S, PACK], BF16, f"x_g{s}") for s in range(PASSES)]
         x_q = [[sbuf([P, HALF], U32, f"x_q{s}_{h}") for h in range(2)] for s in range(PASSES)]
         x_s = [[sbuf([P, HALF], U8, f"x_s{s}_{h}") for h in range(2)] for s in range(PASSES)]
@@ -97,42 +98,38 @@ def tile_picked_schnet_gelu_e_kernel(tc, xT, eT, w1, w3, w2, offs, out):
         def quantize_x(s, h):
             quantize(x_q[s][h][:], x_s[s][h][:], x_g[s][:, h * HALF : (h + 1) * HALF, :])
 
-        def interleave(copy, s, j0, j1, a, b):
-            copy(x_g[s][:, a:b, j0:j1], picked[s][:, j0:j1, a:b].rearrange("p j n -> p n j"))
-
         scalar, vector = nc.scalar.copy, nc.vector.tensor_copy
-        gather(0, 0, 0, S)
-        gather(0, 1, 0, S)
         w1_copy(0)
-        gather(0, 2, 0, S)
+        w1_copy(1)
+        gather(0, 0, 0, S)
         quantize(w1_q[0][:], w1_s[0][:], w1_g[0][:])
+        gather(0, 1, 0, S)
+        quantize(w1_q[1][:], w1_s[1][:], w1_g[1][:])
+        gather(0, 2, 0, S)
         gather(0, 3, 0, S)
-        interleave(scalar, 0, 0, 4, 0, S)
+        nc.scalar.copy(x_g[0][:], picked[:].rearrange("p j n -> p n j"))
         gather(1, 0, 0, S)
         gather(1, 1, 0, S)
         quantize_x(0, 0)
         quantize_x(0, 1)
-        w1_copy(1)
         gather(1, 2, 0, S)
-        interleave(scalar, 1, 0, 2, 0, S)
-        quantize(w1_q[1][:], w1_s[1][:], w1_g[1][:])
         gather(1, 3, 0, HALF)
-        interleave(scalar, 1, 2, 4, 0, HALF)
         gather(1, 3, HALF, S)
-        interleave(vector, 1, 2, 4, HALF, S)
         quantize_x(1, 0)
         quantize_x(1, 1)
 
         def w3_copy(copy, m0, m1):
             copy(permuted(w3_g[:], m0, m1), w3_raw[:, :, PACK * m0 : PACK * m1].rearrange("p j (m t) -> p m t j", t=PACK))
 
-        w3_copy(nc.scalar.copy, 0, 44)
-        w3_copy(nc.vector.tensor_copy, 44, 128)
+        w3_copy(nc.scalar.copy, 0, 64)
+        w3_copy(nc.vector.tensor_copy, 64, 128)
         quantize(w3_q[:], w3_s[:], w3_g[:])
 
-        c_ps = [psum.tile([P, PACK, CHUNK], F32, name=f"c_ps{n}", tag=f"bank{n}") for n in range(CHUNKS)]
+        c_bank = [0, 1, 2, 3]
+        c_ps = {}
 
         def c(n):
+            c_ps[n] = psum.tile([P, PACK, CHUNK], F32, name=f"c_ps{n}", tag=f"bank{c_bank[n]}")
             h, col = n // 2, slice((n % 2) * CHUNK, (n % 2 + 1) * CHUNK)
             for t in range(PACK):
                 m = slice(t * P, (t + 1) * P)
@@ -140,75 +137,68 @@ def tile_picked_schnet_gelu_e_kernel(tc, xT, eT, w1, w3, w2, offs, out):
                     mx(c_ps[n][:, t, :], (w1_q[s][:, m], w1_s[s][:, m]), (x_q[s][h][:, col], x_s[s][h][:, col]),
                        s == 0, s == PASSES - 1)
 
-        def per_chunk(shape, dtype, name):
-            return [sbuf(shape, dtype, f"{name}{n}") for n in range(CHUNKS)]
-
-        e_g = per_chunk([P, CHUNK, PACK], BF16, "e_g")
-        e_q = per_chunk([P, CHUNK], U32, "e_q")
-        e_s = per_chunk([P, CHUNK], U8, "e_s")
-        g_sb = per_chunk([P, CHUNK, PACK], F32, "g_sb")
-        z_g = per_chunk([P, CHUNK, PACK], BF16, "z_g")
-        z_q = per_chunk([P, CHUNK], U32, "z_q")
-        z_s = per_chunk([P, CHUNK], U8, "z_s")
-        o_sb = per_chunk([P, CHUNK], F32, "o_sb")
+        width = [b - a for a, b in PIECES]
+        pieces = range(len(PIECES))
+        e_g = [sbuf([P, w, PACK], BF16, f"e_g{i}") for i, w in enumerate(width)]
+        e_q = [sbuf([P, w], U32, f"e_q{i}") for i, w in enumerate(width)]
+        e_s = [sbuf([P, w], U8, f"e_s{i}") for i, w in enumerate(width)]
+        g_sb = [sbuf([P, w, PACK], F32, f"g_sb{i}") for i, w in enumerate(width)]
+        z_g = [sbuf([P, w, PACK], BF16, f"z_g{i}") for i, w in enumerate(width)]
+        z_q = [sbuf([P, w], U32, f"z_q{i}") for i, w in enumerate(width)]
+        z_s = [sbuf([P, w], U8, f"z_s{i}") for i, w in enumerate(width)]
+        o_sb = [sbuf([P, CHUNK], F32, f"o_sb{n}") for n in range(CHUNKS)]
         w2_g = sbuf([P, N, PACK], BF16, "w2_g")
         w2_q = sbuf([P, N], U32, "w2_q")
         w2_s = sbuf([P, N], U8, "w2_s")
-        f_ps = [psum.tile([P, PACK, CHUNK], F32, name=f"f_ps{n}", tag=f"bank{4 + n}") for n in range(CHUNKS)]
+        f_bank = [2, 3, 4, 5, 6]
+        o_bank = [4, 5, 6, 7, 0]
+        f_ps = {}
 
-        def e_copy(copy, n):
-            per = E_LOAD // CHUNK
-            a = (n % per) * CHUNK
-            copy(e_g[n][:], e_raw[n // per][:, :, a : a + CHUNK].rearrange("p j c -> p c j"))
+        def chunk_cols(i):
+            a = PIECES[i][0] % CHUNK
+            return PIECES[i][0] // CHUNK, slice(a, a + width[i])
 
-        def e_quantize(n):
-            quantize(e_q[n][:], e_s[n][:], e_g[n][:])
+        def e(copy, i):
+            n, cols = chunk_cols(i)
+            copy(e_g[i][:], e_raw[n][:, :, cols].rearrange("p j c -> p c j"))
+            quantize(e_q[i][:], e_s[i][:], e_g[i][:])
 
-        def f(n):
+        def f(i):
+            f_ps[i] = psum.tile([P, PACK, width[i]], F32, name=f"f_ps{i}", tag=f"bank{f_bank[i]}")
             for t in range(PACK):
                 m = slice(t * P, (t + 1) * P)
-                mx(f_ps[n][:, t, :], (w3_q[:, m], w3_s[:, m]), (e_q[n][:], e_s[n][:]), True, True)
+                mx(f_ps[i][:, t, :], (w3_q[:, m], w3_s[:, m]), (e_q[i][:], e_s[i][:]), True, True)
 
-        def gelu(n):
-            nc.scalar.activation(g_sb[n][:], f_ps[n][:].rearrange("p t n -> p n t"), GELU)
+        def gelu(i):
+            nc.scalar.activation(g_sb[i][:], f_ps[i][:].rearrange("p t n -> p n t"), GELU)
 
-        def z(n):
-            nc.vector.tensor_tensor(z_g[n][:], c_ps[n][:].rearrange("p t n -> p n t"), g_sb[n][:], MULT)
+        def z(i):
+            n, cols = chunk_cols(i)
+            nc.vector.tensor_tensor(z_g[i][:], c_ps[n][:, :, cols].rearrange("p t n -> p n t"), g_sb[i][:], MULT)
 
-        def project(copy, n):
-            quantize(z_q[n][:], z_s[n][:], z_g[n][:])
-            o_ps = psum.tile([P, CHUNK], F32, name=f"o_ps{n}", tag=f"bank{n}")
-            mx(o_ps[:], (w2_q[:], w2_s[:]), (z_q[n][:], z_s[n][:]), True, True)
-            copy(o_sb[n][:], o_ps[:])
-            nc.sync.dma_start(out=out[:, n * CHUNK : (n + 1) * CHUNK], in_=o_sb[n][:])
+        def project(copy, i):
+            n, cols = chunk_cols(i)
+            quantize(z_q[i][:], z_s[i][:], z_g[i][:])
+            o_ps = psum.tile([P, width[i]], F32, name=f"o_ps{i}", tag=f"bank{o_bank[i]}")
+            mx(o_ps[:], (w2_q[:], w2_s[:]), (z_q[i][:], z_s[i][:]), True, True)
+            copy(o_sb[n][:, cols], o_ps[:])
+            if PIECES[i][1] % CHUNK == 0:
+                nc.sync.dma_start(out=out[:, n * CHUNK : (n + 1) * CHUNK], in_=o_sb[n][:])
 
-        e_copy(scalar, 0)
-        e_copy(vector, 1)
-        e_quantize(0)
-        e_quantize(1)
+        for i, copy in enumerate((vector, vector, scalar, vector, scalar)):
+            e(copy, i)
         c(0)
         f(0)
-        f(1)
-        c(1)
         gelu(0)
-        e_copy(scalar, 2)
-        e_copy(vector, 3)
-        e_quantize(3)
-        gelu(1)
-        e_quantize(2)
-        f(2)
+        c(1)
+        for i in pieces[1:]:
+            f(i)
+            gelu(i)
         c(2)
-        f(3)
         c(3)
-        z(0)
-        gelu(2)
-        z(1)
-        gelu(3)
+        for i in pieces:
+            z(i)
         vector(w2_g[:], w2_raw[:].rearrange("p j c -> p c j"))
         quantize(w2_q[:], w2_s[:], w2_g[:])
-        z(2)
-        project(scalar, 0)
-        project(scalar, 1)
-        z(3)
-        project(scalar, 2)
-        project(vector, 3)
+        for i in pieces:
+            project(scalar if i < 4 else vector, i)

@@ -3,7 +3,7 @@ from contextlib import ExitStack
 import concourse.mybir as mybir
 
 K, T, S, J, H, N = 1024, 2048, 512, 512, 512, 128
-FLOPS = 2 * (K * H * S + J * H * S + H * N * S)
+FLOPS = 2 * S * (K * H + J * H + H * N)
 
 F32 = mybir.dt.float32
 BF16 = mybir.dt.bfloat16
@@ -17,15 +17,21 @@ MULT = mybir.AluOpType.mult
 P = 128
 PACK = 4
 PASSES = K // (P * PACK)
+PER_OFFSET_COLUMN = 16
 HALF = S // 2
 CHUNK = 128
-CHUNKS = S // CHUNK
-E_LOAD = 128
+
+E_LOADS = [(0, 256), (256, 384), (384, 512)]
 PIECES = [(0, 64), (64, 128), (128, 256), (256, 384), (384, 512)]
+C_BANK = [0, 1, 2, 3]
+F_BANK = [2, 3, 4, 5, 6]
+OUT_BANK = [4, 5, 6, 7, 0]
 
 
 def tile_picked_schnet_gelu_e_kernel(tc, xT, eT, w1, w3, w2, offs, out):
     nc = tc.nc
+    scalar_copy, vector_copy = nc.scalar.copy, nc.vector.tensor_copy
+
     with ExitStack() as ctx:
         keep = ctx.enter_context(tc.tile_pool(name="keep", bufs=1))
         psum = ctx.enter_context(tc.psum_pool(name="psum", bufs=1))
@@ -33,172 +39,173 @@ def tile_picked_schnet_gelu_e_kernel(tc, xT, eT, w1, w3, w2, offs, out):
         def sbuf(shape, dtype, name):
             return keep.tile(shape, dtype, name=name, align_bytes=64)
 
-        lists = keep.tile([P, S // 16], U16, name="lists")
+        def codes_and_scales(width, name):
+            return sbuf([P, width], U32, name + "_codes"), sbuf([P, width], U8, name + "_scales")
 
-        warm = sbuf([P, 2], F32, "warm")
-        nc.vector.memset(warm[:], 0.0)
-        warm_out = sbuf([P, 2], F32, "warm_out")
-        nc.scalar.activation(warm_out[:], warm[:], GELU)
+        def grouped(width, name):
+            return sbuf([P, width, PACK], BF16, name)
 
-        def rows(ap, s):
+        lists = keep.tile([P, S // PER_OFFSET_COLUMN], U16, name="lists")
+
+        zeros = sbuf([P, 2], F32, "zeros")
+        nc.vector.memset(zeros[:], 0.0)
+        gelu_of_zeros = sbuf([P, 2], F32, "gelu_of_zeros")
+        nc.scalar.activation(gelu_of_zeros[:], zeros[:], GELU)
+
+        def pass_rows(ap, s):
             return ap[s * P * PACK : (s + 1) * P * PACK, :].rearrange("(p j) c -> p j c", j=PACK)
 
         w1_raw = [sbuf([P, PACK, H], F32, f"w1_raw{s}") for s in range(PASSES)]
-        planes = {}
-
-        def load_plane(s, j):
-            planes[s, j] = sbuf([P, T], F32, f"x_raw{s}{j}")
-            nc.sync.dma_start(out=planes[s, j][:], in_=rows(xT, s)[:, j, :])
-
-        nc.sync.dma_start(out=w1_raw[0][:], in_=rows(w1, 0))
+        nc.sync.dma_start(out=w1_raw[0][:], in_=pass_rows(w1, 0))
         nc.sync.dma_start(lists[:], offs)
-        nc.sync.dma_start(out=w1_raw[1][:], in_=rows(w1, 1))
+        nc.sync.dma_start(out=w1_raw[1][:], in_=pass_rows(w1, 1))
+        atoms = {}
         for s in range(PASSES):
             for j in range(PACK):
-                load_plane(s, j)
+                atoms[s, j] = sbuf([P, T], F32, f"atoms{s}{j}")
+                nc.sync.dma_start(out=atoms[s, j][:], in_=pass_rows(xT, s)[:, j, :])
         w3_raw = sbuf([P, PACK, H], F32, "w3_raw")
-        nc.sync.dma_start(out=w3_raw[:], in_=rows(w3, 0))
-        e_raw = [sbuf([P, PACK, E_LOAD], F32, f"e_raw{i}") for i in range(S // E_LOAD)]
-        for i in range(S // E_LOAD):
-            nc.sync.dma_start(out=e_raw[i][:], in_=rows(eT, 0)[:, :, i * E_LOAD : (i + 1) * E_LOAD])
+        nc.sync.dma_start(out=w3_raw[:], in_=pass_rows(w3, 0))
+        e_raw = [sbuf([P, PACK, b - a], F32, f"e_raw{a}") for a, b in E_LOADS]
+        for tile, (a, b) in zip(e_raw, E_LOADS):
+            nc.sync.dma_start(out=tile[:], in_=pass_rows(eT, 0)[:, :, a:b])
         w2_raw = sbuf([P, PACK, N], F32, "w2_raw")
-        nc.sync.dma_start(out=w2_raw[:], in_=rows(w2, 0))
+        nc.sync.dma_start(out=w2_raw[:], in_=pass_rows(w2, 0))
 
-        def quantize(codes, scales, grouped):
-            nc.vector.quantize_mx(out=codes.bitcast(FP8X4), scales=scales, in_=grouped.rearrange("p c j -> p (c j)"))
+        def quantize(quantised, values):
+            codes, scales = quantised
+            nc.vector.quantize_mx(out=codes.bitcast(FP8X4), scales=scales, in_=values.rearrange("p c j -> p (c j)"))
 
-        def mx(acc, lhs, rhs, start, stop):
+        def columns(pair, cols):
+            return pair[0][:, cols], pair[1][:, cols]
+
+        def multiply(acc, stationary, moving, start, stop):
             nc.tensor.matmul_mx(
-                out=acc, lhsT=lhs[0].bitcast(FP8X4), lhsT_scale=lhs[1],
-                rhs=rhs[0].bitcast(FP8X4), rhs_scale=rhs[1], start=start, stop=stop,
+                out=acc,
+                lhsT=stationary[0].bitcast(FP8X4),
+                lhsT_scale=stationary[1],
+                rhs=moving[0].bitcast(FP8X4),
+                rhs_scale=moving[1],
+                start=start,
+                stop=stop,
             )
 
-        def permuted(grouped, m0, m1):
-            return grouped.rearrange("p (t m) j -> p m t j", t=PACK)[:, m0:m1, :, :]
+        def block(t):
+            return slice(t * P, (t + 1) * P)
+
+        def round_permuted(copy, values, raw, m0, m1):
+            copy(
+                values[:].rearrange("p (t m) j -> p m t j", t=PACK)[:, m0:m1, :, :],
+                raw[:, :, PACK * m0 : PACK * m1].rearrange("p j (m t) -> p m t j", t=PACK),
+            )
+
+        w1_q = [codes_and_scales(H, f"w1_{s}") for s in range(PASSES)]
+        w1_grouped = [grouped(H, f"w1_grouped{s}") for s in range(PASSES)]
+        picked = sbuf([P, PACK, S], F32, "picked")
+        x_grouped = [grouped(S, f"x_grouped{s}") for s in range(PASSES)]
+        x_q = [[codes_and_scales(HALF, f"x_{s}{h}") for h in range(2)] for s in range(PASSES)]
 
         def gather(s, j, a, b):
-            dst = picked[:, j, a:b] if s == 0 else x_g[s][:, a:b, j]
-            nc.vector.tensor_copy(dst, planes[s, j][:].indirect(lists[:, a // 16 : b // 16]))
+            entries = lists[:, a // PER_OFFSET_COLUMN : b // PER_OFFSET_COLUMN]
+            target = picked[:, j, a:b] if s == 0 else x_grouped[s][:, a:b, j]
+            nc.vector.tensor_copy(target, atoms[s, j][:].indirect(entries))
 
-        w1_q = [sbuf([P, H], U32, f"w1_q{s}") for s in range(PASSES)]
-        w1_s = [sbuf([P, H], U8, f"w1_s{s}") for s in range(PASSES)]
-        w1_g = [sbuf([P, H, PACK], BF16, f"w1_g{s}") for s in range(PASSES)]
+        def quantize_atoms(s, h):
+            quantize([part[:] for part in x_q[s][h]], x_grouped[s][:, h * HALF : (h + 1) * HALF, :])
 
-        def w1_copy(s):
-            nc.scalar.copy(permuted(w1_g[s][:], 0, 128), w1_raw[s][:].rearrange("p j (m t) -> p m t j", t=PACK))
-
-        picked = sbuf([P, PACK, S], F32, "picked")
-        x_g = [sbuf([P, S, PACK], BF16, f"x_g{s}") for s in range(PASSES)]
-        x_q = [[sbuf([P, HALF], U32, f"x_q{s}_{h}") for h in range(2)] for s in range(PASSES)]
-        x_s = [[sbuf([P, HALF], U8, f"x_s{s}_{h}") for h in range(2)] for s in range(PASSES)]
-        w3_g = sbuf([P, H, PACK], BF16, "w3_g")
-        w3_q = sbuf([P, H], U32, "w3_q")
-        w3_s = sbuf([P, H], U8, "w3_s")
-
-        def quantize_x(s, h):
-            quantize(x_q[s][h][:], x_s[s][h][:], x_g[s][:, h * HALF : (h + 1) * HALF, :])
-
-        scalar, vector = nc.scalar.copy, nc.vector.tensor_copy
-        w1_copy(0)
-        w1_copy(1)
-        gather(0, 0, 0, S)
-        quantize(w1_q[0][:], w1_s[0][:], w1_g[0][:])
-        gather(0, 1, 0, S)
-        quantize(w1_q[1][:], w1_s[1][:], w1_g[1][:])
+        for s in range(PASSES):
+            round_permuted(scalar_copy, w1_grouped[s], w1_raw[s], 0, P)
+        for s in range(PASSES):
+            gather(0, s, 0, S)
+            quantize([part[:] for part in w1_q[s]], w1_grouped[s][:])
         gather(0, 2, 0, S)
         gather(0, 3, 0, S)
-        nc.scalar.copy(x_g[0][:], picked[:].rearrange("p j n -> p n j"))
+        scalar_copy(x_grouped[0][:], picked[:].rearrange("p j n -> p n j"))
         gather(1, 0, 0, S)
         gather(1, 1, 0, S)
-        quantize_x(0, 0)
-        quantize_x(0, 1)
+        for h in range(2):
+            quantize_atoms(0, h)
         gather(1, 2, 0, S)
-        gather(1, 3, 0, HALF)
-        gather(1, 3, HALF, S)
-        quantize_x(1, 0)
-        quantize_x(1, 1)
+        for h in range(2):
+            gather(1, 3, h * HALF, (h + 1) * HALF)
+        for h in range(2):
+            quantize_atoms(1, h)
 
-        def w3_copy(copy, m0, m1):
-            copy(permuted(w3_g[:], m0, m1), w3_raw[:, :, PACK * m0 : PACK * m1].rearrange("p j (m t) -> p m t j", t=PACK))
-
-        w3_copy(nc.scalar.copy, 0, 64)
-        w3_copy(nc.vector.tensor_copy, 64, 128)
-        quantize(w3_q[:], w3_s[:], w3_g[:])
-
-        c_bank = [0, 1, 2, 3]
-        c_ps = {}
-
-        def c(n):
-            c_ps[n] = psum.tile([P, PACK, CHUNK], F32, name=f"c_ps{n}", tag=f"bank{c_bank[n]}")
-            h, col = n // 2, slice((n % 2) * CHUNK, (n % 2 + 1) * CHUNK)
-            for t in range(PACK):
-                m = slice(t * P, (t + 1) * P)
-                for s in range(PASSES):
-                    mx(c_ps[n][:, t, :], (w1_q[s][:, m], w1_s[s][:, m]), (x_q[s][h][:, col], x_s[s][h][:, col]),
-                       s == 0, s == PASSES - 1)
+        w3_q = codes_and_scales(H, "w3")
+        w3_grouped = grouped(H, "w3_grouped")
+        round_permuted(scalar_copy, w3_grouped, w3_raw, 0, P // 2)
+        round_permuted(vector_copy, w3_grouped, w3_raw, P // 2, P)
+        quantize([part[:] for part in w3_q], w3_grouped[:])
 
         width = [b - a for a, b in PIECES]
         pieces = range(len(PIECES))
-        e_g = [sbuf([P, w, PACK], BF16, f"e_g{i}") for i, w in enumerate(width)]
-        e_q = [sbuf([P, w], U32, f"e_q{i}") for i, w in enumerate(width)]
-        e_s = [sbuf([P, w], U8, f"e_s{i}") for i, w in enumerate(width)]
-        g_sb = [sbuf([P, w, PACK], F32, f"g_sb{i}") for i, w in enumerate(width)]
-        z_g = [sbuf([P, w, PACK], BF16, f"z_g{i}") for i, w in enumerate(width)]
-        z_q = [sbuf([P, w], U32, f"z_q{i}") for i, w in enumerate(width)]
-        z_s = [sbuf([P, w], U8, f"z_s{i}") for i, w in enumerate(width)]
-        o_sb = [sbuf([P, CHUNK], F32, f"o_sb{n}") for n in range(CHUNKS)]
-        w2_g = sbuf([P, N, PACK], BF16, "w2_g")
-        w2_q = sbuf([P, N], U32, "w2_q")
-        w2_s = sbuf([P, N], U8, "w2_s")
-        f_bank = [2, 3, 4, 5, 6]
-        o_bank = [4, 5, 6, 7, 0]
-        f_ps = {}
+        e_grouped = [grouped(w, f"e_grouped{i}") for i, w in enumerate(width)]
+        e_q = [codes_and_scales(w, f"e_{i}") for i, w in enumerate(width)]
+        filters = [sbuf([P, w, PACK], F32, f"filters{i}") for i, w in enumerate(width)]
+        z_grouped = [grouped(w, f"z_grouped{i}") for i, w in enumerate(width)]
+        z_q = [codes_and_scales(w, f"z_{i}") for i, w in enumerate(width)]
+        out_sb = [sbuf([P, CHUNK], F32, f"out_sb{n}") for n in range(S // CHUNK)]
+        w2_grouped = grouped(N, "w2_grouped")
+        w2_q = codes_and_scales(N, "w2")
+        c_ps, f_ps = {}, {}
 
-        def chunk_cols(i):
-            a = PIECES[i][0] % CHUNK
-            return PIECES[i][0] // CHUNK, slice(a, a + width[i])
+        def place(i):
+            a, b = PIECES[i]
+            n = a // CHUNK
+            return n, slice(a - n * CHUNK, b - n * CHUNK)
 
-        def e(copy, i):
-            n, cols = chunk_cols(i)
-            copy(e_g[i][:], e_raw[n][:, :, cols].rearrange("p j c -> p c j"))
-            quantize(e_q[i][:], e_s[i][:], e_g[i][:])
-
-        def f(i):
-            f_ps[i] = psum.tile([P, PACK, width[i]], F32, name=f"f_ps{i}", tag=f"bank{f_bank[i]}")
+        def product_c(n):
+            c_ps[n] = psum.tile([P, PACK, CHUNK], F32, name=f"c_ps{n}", tag=f"bank{C_BANK[n]}")
+            h, first = divmod(n * CHUNK, HALF)
             for t in range(PACK):
-                m = slice(t * P, (t + 1) * P)
-                mx(f_ps[i][:, t, :], (w3_q[:, m], w3_s[:, m]), (e_q[i][:], e_s[i][:]), True, True)
+                for s in range(PASSES):
+                    moving = columns(x_q[s][h], slice(first, first + CHUNK))
+                    multiply(c_ps[n][:, t, :], columns(w1_q[s], block(t)), moving, s == 0, s == PASSES - 1)
+
+        def quantize_edges(copy, i):
+            a, b = PIECES[i]
+            load = max(k for k in range(len(E_LOADS)) if E_LOADS[k][0] <= a)
+            first = E_LOADS[load][0]
+            copy(e_grouped[i][:], e_raw[load][:, :, a - first : b - first].rearrange("p j c -> p c j"))
+            quantize([part[:] for part in e_q[i]], e_grouped[i][:])
+
+        def product_f(i):
+            f_ps[i] = psum.tile([P, PACK, width[i]], F32, name=f"f_ps{i}", tag=f"bank{F_BANK[i]}")
+            for t in range(PACK):
+                multiply(f_ps[i][:, t, :], columns(w3_q, block(t)), [part[:] for part in e_q[i]], True, True)
 
         def gelu(i):
-            nc.scalar.activation(g_sb[i][:], f_ps[i][:].rearrange("p t n -> p n t"), GELU)
+            nc.scalar.activation(filters[i][:], f_ps[i][:].rearrange("p t n -> p n t"), GELU)
 
-        def z(i):
-            n, cols = chunk_cols(i)
-            nc.vector.tensor_tensor(z_g[i][:], c_ps[n][:, :, cols].rearrange("p t n -> p n t"), g_sb[i][:], MULT)
+        def filter_message(i):
+            n, cols = place(i)
+            c = c_ps[n][:, :, cols].rearrange("p t n -> p n t")
+            nc.vector.tensor_tensor(z_grouped[i][:], c, filters[i][:], MULT)
 
         def project(copy, i):
-            n, cols = chunk_cols(i)
-            quantize(z_q[i][:], z_s[i][:], z_g[i][:])
-            o_ps = psum.tile([P, width[i]], F32, name=f"o_ps{i}", tag=f"bank{o_bank[i]}")
-            mx(o_ps[:], (w2_q[:], w2_s[:]), (z_q[i][:], z_s[i][:]), True, True)
-            copy(o_sb[n][:, cols], o_ps[:])
-            if PIECES[i][1] % CHUNK == 0:
-                nc.sync.dma_start(out=out[:, n * CHUNK : (n + 1) * CHUNK], in_=o_sb[n][:])
+            n, cols = place(i)
+            quantize([part[:] for part in z_q[i]], z_grouped[i][:])
+            out_ps = psum.tile([P, width[i]], F32, name=f"out_ps{i}", tag=f"bank{OUT_BANK[i]}")
+            multiply(out_ps[:], [part[:] for part in w2_q], [part[:] for part in z_q[i]], True, True)
+            copy(out_sb[n][:, cols], out_ps[:])
+            if cols.stop == CHUNK:
+                nc.sync.dma_start(out=out[:, n * CHUNK : (n + 1) * CHUNK], in_=out_sb[n][:])
 
-        for i, copy in enumerate((vector, vector, scalar, vector, scalar)):
-            e(copy, i)
-        c(0)
-        f(0)
+        edge_copies = (scalar_copy, scalar_copy, vector_copy, scalar_copy, vector_copy)
+        for i in pieces:
+            quantize_edges(edge_copies[i], i)
+        product_c(0)
+        product_f(0)
         gelu(0)
-        c(1)
+        product_c(1)
         for i in pieces[1:]:
-            f(i)
+            product_f(i)
             gelu(i)
-        c(2)
-        c(3)
+        product_c(2)
+        product_c(3)
         for i in pieces:
-            z(i)
-        vector(w2_g[:], w2_raw[:].rearrange("p j c -> p c j"))
-        quantize(w2_q[:], w2_s[:], w2_g[:])
+            filter_message(i)
+        vector_copy(w2_grouped[:], w2_raw[:].rearrange("p j c -> p c j"))
+        quantize([part[:] for part in w2_q], w2_grouped[:])
         for i in pieces:
-            project(scalar if i < 4 else vector, i)
+            project(vector_copy if i == pieces[-1] else scalar_copy, i)

from contextlib import ExitStack

import concourse.mybir as mybir

K, T, S, J, H, N = 1024, 2048, 512, 512, 512, 128
FLOPS = 2 * S * (K * H + J * H + H * N)

F32 = mybir.dt.float32
BF16 = mybir.dt.bfloat16
U32 = mybir.dt.uint32
U16 = mybir.dt.uint16
U8 = mybir.dt.uint8
FP8X4 = mybir.dt.float8_e4m3fn_x4
GELU = mybir.ActivationFunctionType.Gelu_apprx_tanh
MULT = mybir.AluOpType.mult

P = 128
PACK = 4
PASSES = K // (P * PACK)
PER_OFFSET_COLUMN = 16
HALF = S // 2
CHUNK = 128

E_LOADS = [(0, 256), (256, 384), (384, 512)]
PIECES = [(0, 64), (64, 128), (128, 256), (256, 384), (384, 512)]
C_BANK = [0, 1, 2, 3]
F_BANK = [2, 3, 4, 5, 6]
OUT_BANK = [4, 5, 6, 7, 0]


def tile_picked_schnet_gelu_e_kernel(tc, xT, eT, w1, w3, w2, offs, out):
    nc = tc.nc
    scalar_copy, vector_copy = nc.scalar.copy, nc.vector.tensor_copy

    with ExitStack() as ctx:
        keep = ctx.enter_context(tc.tile_pool(name="keep", bufs=1))
        psum = ctx.enter_context(tc.psum_pool(name="psum", bufs=1))

        def sbuf(shape, dtype, name):
            return keep.tile(shape, dtype, name=name, align_bytes=64)

        def codes_and_scales(width, name):
            return sbuf([P, width], U32, name + "_codes"), sbuf([P, width], U8, name + "_scales")

        def grouped(width, name):
            return sbuf([P, width, PACK], BF16, name)

        lists = keep.tile([P, S // PER_OFFSET_COLUMN], U16, name="lists")

        zeros = sbuf([P, 2], F32, "zeros")
        nc.vector.memset(zeros[:], 0.0)
        gelu_of_zeros = sbuf([P, 2], F32, "gelu_of_zeros")
        nc.scalar.activation(gelu_of_zeros[:], zeros[:], GELU)

        def pass_rows(ap, s):
            return ap[s * P * PACK : (s + 1) * P * PACK, :].rearrange("(p j) c -> p j c", j=PACK)

        w1_raw = [sbuf([P, PACK, H], F32, f"w1_raw{s}") for s in range(PASSES)]
        nc.sync.dma_start(out=w1_raw[0][:], in_=pass_rows(w1, 0))
        nc.sync.dma_start(lists[:], offs)
        nc.sync.dma_start(out=w1_raw[1][:], in_=pass_rows(w1, 1))
        atoms = {}
        for s in range(PASSES):
            for j in range(PACK):
                atoms[s, j] = sbuf([P, T], F32, f"atoms{s}{j}")
                nc.sync.dma_start(out=atoms[s, j][:], in_=pass_rows(xT, s)[:, j, :])
        w3_raw = sbuf([P, PACK, H], F32, "w3_raw")
        nc.sync.dma_start(out=w3_raw[:], in_=pass_rows(w3, 0))
        e_raw = [sbuf([P, PACK, b - a], F32, f"e_raw{a}") for a, b in E_LOADS]
        for tile, (a, b) in zip(e_raw, E_LOADS):
            nc.sync.dma_start(out=tile[:], in_=pass_rows(eT, 0)[:, :, a:b])
        w2_raw = sbuf([P, PACK, N], F32, "w2_raw")
        nc.sync.dma_start(out=w2_raw[:], in_=pass_rows(w2, 0))

        def quantize(quantised, values):
            codes, scales = quantised
            nc.vector.quantize_mx(out=codes.bitcast(FP8X4), scales=scales, in_=values.rearrange("p c j -> p (c j)"))

        def columns(pair, cols):
            return pair[0][:, cols], pair[1][:, cols]

        def multiply(acc, stationary, moving, start, stop):
            nc.tensor.matmul_mx(
                out=acc,
                lhsT=stationary[0].bitcast(FP8X4),
                lhsT_scale=stationary[1],
                rhs=moving[0].bitcast(FP8X4),
                rhs_scale=moving[1],
                start=start,
                stop=stop,
            )

        def block(t):
            return slice(t * P, (t + 1) * P)

        def round_permuted(copy, values, raw, m0, m1):
            copy(
                values[:].rearrange("p (t m) j -> p m t j", t=PACK)[:, m0:m1, :, :],
                raw[:, :, PACK * m0 : PACK * m1].rearrange("p j (m t) -> p m t j", t=PACK),
            )

        w1_q = [codes_and_scales(H, f"w1_{s}") for s in range(PASSES)]
        w1_grouped = [grouped(H, f"w1_grouped{s}") for s in range(PASSES)]
        picked = sbuf([P, PACK, S], F32, "picked")
        x_grouped = [grouped(S, f"x_grouped{s}") for s in range(PASSES)]
        x_q = [[codes_and_scales(HALF, f"x_{s}{h}") for h in range(2)] for s in range(PASSES)]

        def gather(s, j, a, b):
            entries = lists[:, a // PER_OFFSET_COLUMN : b // PER_OFFSET_COLUMN]
            target = picked[:, j, a:b] if s == 0 else x_grouped[s][:, a:b, j]
            nc.vector.tensor_copy(target, atoms[s, j][:].indirect(entries))

        def quantize_atoms(s, h):
            quantize([part[:] for part in x_q[s][h]], x_grouped[s][:, h * HALF : (h + 1) * HALF, :])

        for s in range(PASSES):
            round_permuted(scalar_copy, w1_grouped[s], w1_raw[s], 0, P)
        for s in range(PASSES):
            gather(0, s, 0, S)
            quantize([part[:] for part in w1_q[s]], w1_grouped[s][:])
        gather(0, 2, 0, S)
        gather(0, 3, 0, S)
        scalar_copy(x_grouped[0][:], picked[:].rearrange("p j n -> p n j"))
        gather(1, 0, 0, S)
        gather(1, 1, 0, S)
        for h in range(2):
            quantize_atoms(0, h)
        gather(1, 2, 0, S)
        for h in range(2):
            gather(1, 3, h * HALF, (h + 1) * HALF)
        for h in range(2):
            quantize_atoms(1, h)

        w3_q = codes_and_scales(H, "w3")
        w3_grouped = grouped(H, "w3_grouped")
        round_permuted(scalar_copy, w3_grouped, w3_raw, 0, P // 2)
        round_permuted(vector_copy, w3_grouped, w3_raw, P // 2, P)
        quantize([part[:] for part in w3_q], w3_grouped[:])

        width = [b - a for a, b in PIECES]
        pieces = range(len(PIECES))
        e_grouped = [grouped(w, f"e_grouped{i}") for i, w in enumerate(width)]
        e_q = [codes_and_scales(w, f"e_{i}") for i, w in enumerate(width)]
        filters = [sbuf([P, w, PACK], F32, f"filters{i}") for i, w in enumerate(width)]
        z_grouped = [grouped(w, f"z_grouped{i}") for i, w in enumerate(width)]
        z_q = [codes_and_scales(w, f"z_{i}") for i, w in enumerate(width)]
        out_sb = [sbuf([P, CHUNK], F32, f"out_sb{n}") for n in range(S // CHUNK)]
        w2_grouped = grouped(N, "w2_grouped")
        w2_q = codes_and_scales(N, "w2")
        c_ps, f_ps = {}, {}

        def place(i):
            a, b = PIECES[i]
            n = a // CHUNK
            return n, slice(a - n * CHUNK, b - n * CHUNK)

        def product_c(n):
            c_ps[n] = psum.tile([P, PACK, CHUNK], F32, name=f"c_ps{n}", tag=f"bank{C_BANK[n]}")
            h, first = divmod(n * CHUNK, HALF)
            for t in range(PACK):
                for s in range(PASSES):
                    moving = columns(x_q[s][h], slice(first, first + CHUNK))
                    multiply(c_ps[n][:, t, :], columns(w1_q[s], block(t)), moving, s == 0, s == PASSES - 1)

        def quantize_edges(copy, i):
            a, b = PIECES[i]
            load = max(k for k in range(len(E_LOADS)) if E_LOADS[k][0] <= a)
            first = E_LOADS[load][0]
            copy(e_grouped[i][:], e_raw[load][:, :, a - first : b - first].rearrange("p j c -> p c j"))
            quantize([part[:] for part in e_q[i]], e_grouped[i][:])

        def product_f(i):
            f_ps[i] = psum.tile([P, PACK, width[i]], F32, name=f"f_ps{i}", tag=f"bank{F_BANK[i]}")
            for t in range(PACK):
                multiply(f_ps[i][:, t, :], columns(w3_q, block(t)), [part[:] for part in e_q[i]], True, True)

        def gelu(i):
            nc.scalar.activation(filters[i][:], f_ps[i][:].rearrange("p t n -> p n t"), GELU)

        def filter_message(i):
            n, cols = place(i)
            c = c_ps[n][:, :, cols].rearrange("p t n -> p n t")
            nc.vector.tensor_tensor(z_grouped[i][:], c, filters[i][:], MULT)

        def project(copy, i):
            n, cols = place(i)
            quantize([part[:] for part in z_q[i]], z_grouped[i][:])
            out_ps = psum.tile([P, width[i]], F32, name=f"out_ps{i}", tag=f"bank{OUT_BANK[i]}")
            multiply(out_ps[:], [part[:] for part in w2_q], [part[:] for part in z_q[i]], True, True)
            copy(out_sb[n][:, cols], out_ps[:])
            if cols.stop == CHUNK:
                nc.sync.dma_start(out=out[:, n * CHUNK : (n + 1) * CHUNK], in_=out_sb[n][:])

        edge_copies = (scalar_copy, scalar_copy, vector_copy, scalar_copy, vector_copy)
        for i in pieces:
            quantize_edges(edge_copies[i], i)
        product_c(0)
        product_f(0)
        gelu(0)
        product_c(1)
        for i in pieces[1:]:
            product_f(i)
            gelu(i)
        product_c(2)
        product_c(3)
        for i in pieces:
            filter_message(i)
        vector_copy(w2_grouped[:], w2_raw[:].rearrange("p j c -> p c j"))
        quantize([part[:] for part in w2_q], w2_grouped[:])
        for i in pieces:
            project(vector_copy if i == pieces[-1] else scalar_copy, i)
